import numpy as np, ml_dtypes
CORES = [5,29,101,125,133,157,229,253]
N = 8
BF = ml_dtypes.bfloat16
def gentries(a):
    return np.ascontiguousarray(a.reshape(8, 16, -1).transpose(0, 2, 1)).reshape(8, -1)
def gtable(e):
    e = np.asarray(e); return np.ascontiguousarray(e.reshape(8, -1, 16).transpose(0, 2, 1)).reshape(128, -1).astype(np.int32)
V, W, D, RO = 512, 4096, 16, 3
U = N * V
def family(rng):
    share = rng.permutation(np.array([1.0, 1.0, 1.0, 0.97, 0.95, 0.9, 0.6, 0.0])).reshape(8, 1, 1)
    q = rng.choice(np.array([2, 3, 4, 6]), (8, 16, 1)); often = rng.integers(0, 256, (8, 16, 8))
    v = np.take_along_axis(often, (rng.random((8, 16, W)) * q).astype(np.int64), 2)
    return np.where(rng.random((8, 16, W)) < share, v, rng.integers(0, 256, (8, 16, W)))
def parts(rng):
    return family(rng), rng.integers(0, 4096, (N, 8, V)), rng.integers(0, U, (N, 8, D, V))
def pack(f, c, e):
    return {"fam": np.ascontiguousarray(np.broadcast_to(f.reshape(1, 128, W), (N, 128, W))).astype(np.float32).astype(BF),
            "c0": np.stack([gtable(a) for a in c]), "nb": np.stack([gtable(a.reshape(8, -1)) for a in e])}
def setup_inputs(rng):
    return pack(*parts(rng))
def setup_inputs_ties(rng):
    f, c, e = parts(rng); f[:, 8:] = f[:, :8]; g = rng.permutation(8)
    f[g[0]] = rng.integers(0, 3, (1, W)); f[g[1]] = rng.integers(1, 256)
    return pack(f, c, e)
def setup_inputs_ends(rng):
    f, c, e = parts(rng); v = np.arange(V)[None, :]; a = int(rng.integers(0, N)); b = (a + 1) % N
    for r in range(N):
        e[r, 0] = rng.choice(np.array([0, U - 1, V - 1, V]), (D, V))
        e[r, 1] = np.where(rng.random((D, V)) < 0.5, r * V + v, e[r, 1]); e[r, 2] = e[r, 2, :1]
        e[r, 3] = ((r + 1) % N) * V + rng.integers(0, V, (D, V)); e[r, 4] = (r * V + v + 1 + np.arange(D)[:, None]) & (U - 1)
    e[:, 2] = b * V + (e[:, 2] & (V - 1)); e[:, 5] = b * V + int(rng.integers(0, V)); e[a] = b * V + (e[a] & (V - 1))
    c[:, 5:7] = rng.choice(np.array([0, 1, W - 1, 4094, 4095]), (N, 2, V))
    f[5] = 100 * rng.integers(0, 3, (16, W))
    f[6] = rng.integers(0, 256); f[6, 15] = np.where(rng.random(W) < 0.3, 255, rng.integers(0, 256, W))
    f[7] = rng.choice(np.array([0, 255]), (16, W)); c[:, :, 0] = 4095; c[:, :, V - 1] = 0
    c[:, 3] = (rng.permutation(U) & 4095).reshape(N, V); c[:, 4] = rng.integers(0, 4096)
    return pack(f, c, e)
def setup_inputs_same(rng):
    f, c, e = parts(rng); g = (int(rng.integers(0, 8)) + np.arange(8)) & 7
    c[:, g[0]] = rng.integers(0, 4096); c[:, g[1]] = rng.integers(0, 4096)
    c[:, g[2]] = rng.choice(rng.integers(0, 4096, 2), (N, V)); c[:, g[3]] = rng.integers(0, 4096, (N, 1))
    for i in (g[4], g[5]): f[i] = f[i][:, (np.arange(W) >> 3) << 3]
    return pack(f, c, e)
def setup_inputs_still(rng):
    f, c, e = parts(rng); c[:] = rng.integers(0, 4096, (1, 8, 1)); g = int(rng.integers(0, 8))
    for m in (g, (g + 4) & 7):
        h = (m + 7) & 7; one = int(c[0, m, 0]); two = one ^ (W >> 1); before = int(c[0, h, 0]); after = int(c[0, (m + 1) & 7, 0])
        o = rng.permutation(U); s = np.zeros(U, np.int64); s[o[U // 2:]] = 1
        e[:, m] = o[(e[:, m] & (U // 2 - 1)) + (U // 2) * s.reshape(N, 1, V)]
        c[:, m] = np.where(s == 1, two, one).reshape(N, V)
        f[h] = rng.integers(0, 256, (16, W)); f[m] = rng.integers(0, 256, (16, W))
        f[h, :, (before + two) & (W - 1)] = f[h, :, (before + one) & (W - 1)]
        f[m, 0, (two + after) & (W - 1)] = (int(f[m, 0, (one + after) & (W - 1)]) + int(rng.integers(1, 256))) & 255
    return pack(f, c, e)
def setup_inputs_spread(rng):
    ex = rng.permutation(np.array([1.0, 2.0, 4.0, 8.0, 20.0, 60.0, 200.0, 400.0])).reshape(8, 1, 1)
    f = (256 * rng.random((8, 16, W)) ** ex).astype(np.int64); up = rng.random((8, 16, 1)) < 0.5; f = np.where(up, 255 - f, f)
    c = (4096 * rng.random((N, 8, V)) ** rng.choice(np.array([1.0, 3.0, 6.0]), (N, 8, 1))).astype(np.int64)
    e = (U * rng.random((N, 8, D, V)) ** rng.choice(np.array([1.0, 2.0, 5.0]), (N, 8, D, 1))).astype(np.int64)
    return pack(f, c, e)
def check_inputs(d):
    bad = []
    for k, lo, hi in (("c0", 0, 4095), ("nb", 0, U - 1)):
        if np.min(d[k]) < lo or np.max(d[k]) > hi: bad.append("range of " + k)
    m = np.asarray(d["fam"]).astype(np.float32)
    if not np.all((m >= 0) & (m <= 255) & (m == np.floor(m))): bad.append("numbers of fam")
    if not np.all(m == m[:1]): bad.append("fam alike on all ranks")
    return bad
def reference(fam, c0, nb):
    f = fam.astype(np.float32).astype(np.int16).reshape(N, 8, 16, W)
    c = np.stack([gentries(a) for a in c0]).astype(np.int64)
    e = np.stack([gentries(a) for a in nb]).astype(np.int64).reshape(N, 8, D, V)
    k = np.arange(D)[:, None]
    for t in range(RO):
        ct = np.ascontiguousarray(c.transpose(1, 0, 2)).reshape(8, 1, U)
        look = (ct + np.roll(ct, -1, axis=0) + 1021 * t) & (W - 1)
        nc, ne, nx = [], [], []
        for a in range(N):
            p = np.take_along_axis(f[a], look, 2)
            own = p[:, :, a * V:(a + 1) * V]
            eq = np.take_along_axis(p, e[a].reshape(8, 1, D * V), 2).reshape(8, 16, D, V) == own[:, :, None, :]
            cnt = np.add.reduce(eq, axis=2, dtype=np.int64)
            x = np.argmin(cnt, axis=1)
            new = 256 * x + np.take_along_axis(own, x[:, None, :], 1)[:, 0].astype(np.int64)
            stay = np.take_along_axis(eq, x[:, None, None, :], 1)[:, 0]
            nc.append(new); nx.append(np.take_along_axis(cnt, x[:, None, :], 1)[:, 0])
            ne.append(np.where(stay, e[a], (37 * e[a] + 101 * new[:, None, :] + 811 * k + t) & (U - 1)))
        c = np.stack(nc); e = np.stack(ne); ex = np.stack(nx)
    return {"yc": np.stack([gtable(a) for a in c]).astype(np.float32), "yn": np.stack([gtable(a.reshape(8, -1)) for a in e]).astype(np.float32),
            "yx": np.stack([gtable(a) for a in ex]).astype(np.float32)}

from concourse.bass import DstId, RemoteDMATransfer
from concourse.mybir import AluOpType as A, ActivationFunctionType as F

N, RO = 8, 3
COLS = True
NS_K = {(0, 0): 10, (0, 1): 12, (1, 0): 10, (1, 1): 12, (2, 0): 10, (2, 1): 14}
W_NE, W_P, W_NP, W_I, W_D = 16, 17, 18, 19, 20

SCRATCH = {}
for _dt, _list in (
        ("bfloat16", (("famb", 4096), ("pt0", 4096), ("pt1", 4096), ("pt2", 4096), ("ow", 512), ("eq", 8192), ("wt", 21 * 128),
                      ("ckb", 512), ("ones", 256))),
        ("int32", (("ca", 32), ("cb", 32), ("l0", 32), ("l1", 32), ("ei", 512), ("xi", 512), ("ui", 512), ("ns", 512), ("ki", 32),
                   ("km", 32), ("o1", 32), ("o2", 32), ("o3", 32), ("ji", 192), ("jj", 192), ("qi", 16), ("qp", 16), ("qb", 16),
                   ("cki", 256), ("ckt", 512))),
        ("float32", (("ef", 512), ("y1", 512), ("xk", 512), ("tr", 1024), ("sc", 1024), ("kf", 32), ("yco", 32), ("yxo", 32),
                     ("w36", 128), ("jf", 192), ("j2", 160), ("sw", 320), ("lm", 320), ("qf", 8), ("rs", 256), ("pw", 256))),
        ("uint16", (("nbu", 512), ("bo", 16), ("lk0", 256), ("lk1", 256), ("lk2", 256)))):
    for _name, _w in _list:
        SCRATCH[_name] = ("sbuf", [128, _w], _dt)
SCRATCH["nb0"] = ("sbuf", [128, 16, 32], "int32")
SCRATCH["yno"] = ("sbuf", [128, 16, 32], "float32")
for _name in ("pown", "pkey0", "pkey1", "pmsk0", "pmsk1", "psw", "pbb0", "pbb1"):
    SCRATCH[_name] = ("psum", [128, 512], "float32")

EVENTS = [(0, 0), (1, 0), (1, 1), (2, 0), (2, 1)]
SEMAPHORES = (["V", "S", "PE", "G", "sent", "dca", "dcb", "dcc", "dfam", "dnb", "dyc", "dyx", "dyn", "dow0", "dow1", "dow2"]
              + ["a%d%d_%d" % (t, h, r) for t, h in EVENTS for r in range(N)])


def first_col(r, h):
    return 16 * ((1 - r % 2) if h == 0 else r % 2)


def columns(t, h):
    return COLS and t > 0 and h == 0


def slot(t, h, r):
    if t == 0:
        return 32 * r, 32 * r + 32
    a = 32 * r + first_col(r, h)
    return a, a + 16


def piece(T, t, h, r):
    a, b = slot(t, h, r)
    return T["pt%d" % t][:, 16 * a:16 * b] if columns(t, h) else T["lk%d" % t][:, a:b]


def piece_name(t, h, r):
    return ("p%d%d_%d" if columns(t, h) else "lk%d%d_%d") % (t, h, r)


def routes(core, T, topo):
    near = [d for d in T.cores if d != core and topo.may_write(core, d)]
    far = [d for d in T.cores if d != core and not topo.may_write(core, d)]
    able = [c for c in topo.cores_of(core) if c != core and all(topo.may_write(c, d) for d in far)]
    return near, far, {False: [c for c in able if topo.die(c) == topo.die(core)][:2],
                       True: [c for c in able if topo.die(c) != topo.die(core)][:2]}


def bits(engines):
    m = 0
    for e in engines:
        m |= 1 << e
    return m


def dst_id(topo, dst, src):
    rid, pid = topo.addr(dst, src)
    return DstId(rid=rid, pnc=pid)


def relay_program(g, core, T, topo):
    for owner in T.cores:
        near, far, relays = routes(owner, T, topo)
        r = T.rank_of(owner)
        total = 0
        for t, h in EVENTS:
            rel = relays[columns(t, h)]
            if core not in rel:
                continue
            mine = far[rel.index(core)::len(rel)]
            n = len(topo.engines(core, mine[0]))
            ap = piece(T, t, h, r)
            sem = T.sem["a%d%d_%d" % (t, h, r)]
            g.wait_ge(sem, n)
            g.remote_dma_fused([RemoteDMATransfer(dst_ids=[dst_id(topo, d, core) for d in mine],
                                                  dma_engine_mask=topo.mask(core, mine[0]), remote_sem=sem,
                                                  srcs=[ap], dsts=[ap for d in mine])], local_sem=T.sem.sent)
            total += n
        if total:
            g.wait_ge(T.sem.sent, total)


def run_ops(ops, outside, queues, T):
    writer, readers, banker = dict(outside), {}, {}
    clock = {q: {} for q in queues}
    index = {q: 0 for q in queues}
    stamp, plan, marked = {}, [], set()
    for q, fn, rd, wr, banks, own in ops:
        deps = [writer[b] for b in rd + wr if b in writer]
        for b in wr:
            deps.extend(readers.get(b, []))
        deps.extend(banker[b] for b in banks if b in banker and banker[b][0] != q)
        need = {}
        for key, val in deps:
            if not (key == q and q == "PE") and clock[q].get(key, 0) < val:
                need[key] = max(need.get(key, 0), val)
        waits = []
        for key, val in sorted(need.items(), key=lambda kv: kv[0] != q):
            if clock[q].get(key, 0) >= val:
                continue
            waits.append((key, val))
            clock[q][key] = val
            for k2, v2 in stamp.get((key, val), {}).items():
                if clock[q].get(k2, 0) < v2:
                    clock[q][k2] = v2
            if key in queues:
                marked.add((key, val))
        if own is None:
            index[q] += 1
        me = own or (q, index[q])
        stamp[me] = dict(clock[q])
        for b in rd:
            readers.setdefault(b, []).append(me)
        for b in wr:
            writer[b] = me
            readers[b] = []
        for b in banks:
            banker[b] = me
        plan.append((q, fn, waits, me, own))
    count = {}
    for q in queues:
        for n, val in enumerate(sorted(v for k, v in marked if k == q)):
            count[(q, val)] = n + 1
    for q, fn, waits, me, own in plan:
        for key, val in waits:
            queues[q].wait_ge(T.sem[key], count.get((key, val), val))
        ins = fn()
        if own is not None:
            if ins is not None:
                ins.then_inc(T.sem[own[0]], own[1])
        elif me in marked:
            ins.then_inc(T.sem[q], 1)


def rank_program(g, core, T, topo):
    r = T.rank_of(core)
    if r is None:
        relay_program(g, core, T, topo)
        return
    near, far, relays = routes(core, T, topo)
    V, S, PE, SP = g.vector, g.scalar, g.tensor, g.sync
    ops = []
    off = topo.engines(core, near[0])
    outside = {piece_name(t, h, q): ("a%d%d_%d" % (t, h, q), len(off)) for t, h in EVENTS for q in range(N) if q != r}

    def op(q, fn, rd, wr, banks=(), own=None):
        ops.append((q, fn, list(rd), list(wr), list(banks), own))

    def ts(out, in0, s1, o0, rd, wr, s2=None, o1=None, banks=()):
        if o1 is None:
            op("V", lambda: V.tensor_scalar(out, in0, s1, None, o0), rd, wr, banks)
        else:
            op("V", lambda: V.tensor_scalar(out, in0, s1, s2, o0, o1), rd, wr, banks)

    def tt(out, in0, in1, o, rd, wr, banks=()):
        op("V", lambda: V.tensor_tensor(out, in0, in1, o), rd, wr, banks)

    def cp(out, in_, rd, wr, banks=()):
        op("V", lambda: V.tensor_copy(out, in_), rd, wr, banks)

    def act(out, in_, rd, wr, banks=(), scale=1.0, bias=0.0):
        if bias:
            op("S", lambda: S.activation(out, in_, F.Identity, bias=bias, scale=scale), rd, wr, banks)
        else:
            op("S", lambda: S.activation(out, in_, F.Copy, scale=scale), rd, wr, banks)

    def mm(out, lhsT, rhs, start, stop, rd, wr, bank):
        op("PE", lambda: PE.matmul(out, lhsT, rhs, start, stop), rd, wr, [bank])

    def w(i):
        return T.wt[:, 128 * i:128 * i + 128]

    def hs(h):
        return slice(256 * h, 256 * h + 256)

    def cs(h):
        return slice(first_col(r, h), first_col(r, h) + 16)

    def ps(name, h):
        return T["p%s%d" % (name, h)][:, 0:256]

    def steps(*fs):
        for f in fs:
            f()

    ident = T.jf[:, 16:144]
    sends = [0]

    def send(t, h):
        ap = piece(T, t, h, r)
        sem = T.sem["a%d%d_%d" % (t, h, r)]
        rel = relays[columns(t, h)]
        rest = [e for e in topo.engines(core, rel[0]) if e not in off]

        def go():
            g.remote_dma_fused([RemoteDMATransfer(dst_ids=[dst_id(topo, c, core)], dma_engine_mask=bits(m), remote_sem=sem,
                                                  src=ap, dst=ap) for c, m in zip(rel, (rest, off))],
                               local_sem=T.sem.sent)
            g.remote_dma_fused([RemoteDMATransfer(dst_ids=[dst_id(topo, d, core) for d in near], dma_engine_mask=bits(off),
                                                  remote_sem=sem, srcs=[ap], dsts=[ap for d in near])],
                               local_sem=T.sem.sent)
        sends[0] += len(rest) + 2 * len(off)
        op("G", go, [piece_name(t, h, r)], [], own=("sent", -sends[0]))

    op("SP", lambda: SP.dma_start(T.ca[:], T.c0[:]), [], ["ca"], own=("dca", 16))
    op("S", lambda: S.dma_start(T.cb[0:112, :], T.c0[16:128, :]), [], ["cb1"], own=("dcb", 16))
    op("SP", lambda: SP.dma_start(T.cb[112:128, :], T.c0[0:16, :]), [], ["cb2"], own=("dcc", 16))
    op("SP", lambda: SP.dma_start(T.famb[:], T.fam[:]), [], ["fam"], own=("dfam", 16))
    op("S", lambda: S.dma_start(T.nb0[:], T.nb[:]), [], ["nb0"], own=("dnb", 16))
    op("G", lambda: g.iota(T.ji[:], [[1, 192]], 240, -1), [], ["ji"])
    op("G", lambda: g.iota(T.qi[:], [[0, 16]], 0, 1), [], ["qi"])
    op("G", lambda: g.iota(T.cki[:], [[811, 16], [0, 16]], 0, 0), [], ["cki"])
    op("V", lambda: V.memset(T.ones[:], 1.0), [], ["ones"])
    op("V", lambda: V.memset(T.rs[:], 0.0), [], ["rs"])
    ts(T.jj[:], T.ji[:], 127, A.bitwise_and, ["ji"], ["jj"])
    op("V", lambda: V.memset(T.rs[:, 0:256:16], float(2 ** 26)), [], ["rs"])
    ts(T.jf[:], T.jj[:], 0.0, A.is_equal, ["jj"], ["jf"])
    ts(T.qp[:], T.qi[:], 15, A.bitwise_and, ["qi"], ["qp"])
    for k in range(16):
        act(w(k), ident, ["jf"], ["w%d" % k], scale=float(2 ** k))
    tt(T.l0[:], T.ca[:], T.cb[:], A.add, ["ca", "cb1", "cb2"], ["l00", "l01"])
    ts(T.l1[:], T.l0[:], 4095, A.bitwise_and, ["l00", "l01"], ["l10", "l11"])
    cp(T.lk0[:, 32 * r:32 * r + 32], T.l1[:], ["l10", "l11"], ["lk00_%d" % r])
    send(0, 0)
    ts(T.qb[:], T.qi[:], 4, A.logical_shift_right, ["qi"], ["qb"], 1, A.bitwise_and)
    ts(T.qf[:, 0:1], T.qp[:, 0:1], 65536.0, A.mult, ["qp"], ["qf0"])
    cp(T.bo[:], T.qp[:], ["qp"], ["bo"])
    ts(T.qf[:, 2:3], T.qb[:, 0:1], 1.0 / 256, A.mult, ["qb"], ["qf2"])
    ts(T.qf[:, 1:2], T.qb[:, 0:1], -1.0 / 256, A.mult, ["qb"], ["qf1"], 1.0 / 256, A.add)
    tt(T.j2[:], T.jf[:, 0:160], T.jf[:, 16:176], A.add, ["jf"], ["j2"])
    for i, s in ((W_NE, -float(2 ** 20)), (W_P, 256.0), (W_NP, -256.0), (W_I, 1.0)):
        act(w(i), ident, ["jf"], ["w%d" % i], scale=s)
    act(T.w36[:], ident, ["jf"], ["w36"], scale=36.0)
    ts(w(W_D), ident, T.qf[:, 0:1], A.mult, ["jf", "qf0"], ["w%d" % W_D])
    for c0 in range(2):
        ts(T.sw[:, 160 * c0:160 * c0 + 160], T.jf[:, 0:160], T.qf[:, 1 + c0:2 + c0], A.mult, ["jf", "qf%d" % (1 + c0)], ["sw%d" % c0])
        ts(T.lm[:, 160 * c0:160 * c0 + 160], T.j2[:], T.qf[:, 1 + c0:2 + c0], A.mult, ["j2", "qf%d" % (1 + c0)], ["lm%d" % c0])
    ts(T.ckt[:, 0:256], T.cki[:], 255, A.bitwise_and, ["cki"], ["ck0"])
    ts(T.ckt[:, 256:512], T.cki[:], 0xF00, A.bitwise_and, ["cki"], ["ck1"])
    for k in range(16):
        op("V", lambda k=k: V.memset(T.pw[:, 16 * k:16 * k + 16], float(2 ** (15 - k))), [], ["pw%d" % k])
    cp(T.ckb[:], T.ckt[:], ["ck0", "ck1"], ["ckb"])
    for h in range(2):
        cp(T.nbu[:, hs(h)], T.nb0[:, :, cs(h)], ["nb0"], ["nbu%d" % h])
        cp(T.ef[:, hs(h)], T.nb0[:, :, cs(h)], ["nb0"], ["ef%d" % h])
    pw_all = ["pw%d" % k for k in range(16)]

    def window(t):
        return T["pt%d" % t][:, 0:4096], ["p%d%d_%d" % (t, h, q) for h in range(2) for q in range(N)]

    def table(q, t, h, x, y=None):
        y = x if y is None else y
        a, b = slot(t, h, x)[0], slot(t, h, y)[1]
        src = T.famb[:, 0:4096].indirect(T["lk%d" % t][:, a:b])
        out = T["pt%d" % t][:, 16 * a:16 * b]
        rd = ["fam", "lk%d%d_%d" % (t, h, x), "lk%d%d_%d" % (t, h, y)]
        wr = ["p%d%d_%d" % (t, h, x), "p%d%d_%d" % (t, h if t else 1, y)]
        (act if q == "S" else cp)(out, src, rd, wr)

    def own_columns(t):
        both = ["p%d0_%d" % (t, r), "p%d1_%d" % (t, r)]
        whole = T["pt%d" % t][:, 512 * r:512 * r + 512]
        op("SP", lambda: SP.dma_start(T.ow[:], whole), both, ["ow"], own=("dow%d" % t, 16))
        mm(T.pown[:], w(W_I), whole, True, True, both + ["w%d" % W_I], ["pown"], "b_own")

    def mine(buf, h, base=0):
        a = base + 16 * first_col(r, h)
        return buf[:, a:a + 256]

    def open_sums(t, h):
        both = ["p%d0_%d" % (t, r), "p%d1_%d" % (t, r)]
        own = mine(T["pt%d" % t], h, 512 * r)
        mm(ps("key", h), w(W_P), own, True, False, both + ["w%d" % W_P], ["key%d" % h], "b_key%d" % h)
        mm(ps("key", h), w(W_D), T.ones[:], False, False, ["ones", "w%d" % W_D], ["key%d" % h], "b_key%d" % h)
        if (t, h) == (RO - 1, 1):
            mm(ps("msk", h), w(W_D), T.ones[:], True, False, ["ones", "w%d" % W_D], ["msk%d" % h], "b_msk%d" % h)
        else:
            mm(ps("msk", h), w(W_NP), own, True, False, both + ["w%d" % W_NP], ["msk%d" % h], "b_msk%d" % h)

    def open_ends(h):
        mm(ps("bb", h), T.w36[:], T.ef[:, hs(h)], True, False, ["w36", "ef%d" % h], ["bb%d" % h], "b_bb%d" % h)
        mm(ps("bb", h), w(W_I), T.ckb[:, 0:256], False, False, ["ckb"], ["bb%d" % h], "b_bb%d" % h)
        mm(ps("bb", h), w(W_I), T.ckb[:, 256:512], False, False, ["ckb"], ["bb%d" % h], "b_bb%d" % h)

    def ends(t, h, n_s, fill, lead, whole=False):
        n_v = 16 - n_s
        fused, rest = list(range(n_v)), list(range(n_v, 16))
        order = fused[:lead]
        fused = fused[lead:]
        while rest or fused:
            order += rest[:2] + fused[:1]
            rest, fused = rest[2:], fused[1:]
        win, p_all = window(t)
        for j, k in enumerate(order):
            steps(*fill.get(j, []))
            c = 256 * h + 16 * k
            e = T.eq[:, 16 * c:16 * c + 256]
            name = "eq%d_%d" % (h, k)
            if k < n_v:
                tt(e, win.indirect(T.nbu[:, c:c + 16]), mine(T.ow, h), A.not_equal, p_all + ["ow", "nbu%d" % h], [name])
            else:
                tt(e, e, mine(T.pown, h), A.not_equal, [name, "pown"], [name], ["b_own"])
            mm(ps("key", h), w(W_NE), e, False, j == 15, [name, "w%d" % W_NE], ["key%d" % h], "b_key%d" % h)
            if whole:
                mm(ps("msk", h), w(W_NE), e, False, False, [name], ["msk%d" % h], "b_msk%d" % h)
            mm(ps("msk", h), w(k), e, False, whole and j == 15, [name, "w%d" % k], ["msk%d" % h], "b_msk%d" % h)

    def gathers(t, h, n_s, a, b):
        win, p_all = window(t)
        for k in list(range(16 - n_s, 16, 2))[a:b]:
            c = 256 * h + 16 * k
            act(T.eq[:, 16 * c:16 * c + 512], win.indirect(T.nbu[:, c:c + 32]), p_all + ["nbu%d" % h],
                ["eq%d_%d" % (h, k), "eq%d_%d" % (h, k + 1)])

    def least(h, q):
        c = slice(512 * h + 256 * q, 512 * h + 256 * q + 256)
        nm = ("key", "msk")[q]
        op("V", lambda: V.transpose(T.tr[:, c], ps(nm, h)), ["%s%d" % (nm, h)], ["tr%d%d" % (h, q)], ["b_%s%d" % (nm, h)])
        return lambda: op("V", lambda: V.tensor_tensor_scan(T.sc[:, c], T.rs[:], T.tr[:, c], 0.0, A.add, A.min),
                          ["rs", "tr%d%d" % (h, q)], ["sc%d%d" % (h, q)])

    def key2(h):
        act(T.xk[:, hs(h)], ps("key", h), ["key%d" % h], ["xk%d" % h], ["b_key%d" % h])
        return lambda: mm(ps("msk", h), ident, T.xk[:, hs(h)], False, True, ["xk%d" % h, "jf"], ["msk%d" % h], "b_msk%d" % h)

    def back(mat, h):
        nq, base, name = (1, 64 * h, "lp%d" % h) if mat == "lm" else (2, 64 * h + 16, "kp%d" % h)
        for c0 in range(2):
            for g0 in range(2):
                a = 160 * c0 + 16 - 16 * (g0 - c0)
                mm(T.psw[:, base + c0:base + 16 * nq:2], T[mat][:, a:a + 128],
                   T.sc[:, 512 * h + 16 * g0 + 15:512 * h + 256 * nq:32], g0 == 0, g0 == 1,
                   ["%s%d" % (mat, c0)] + ["sc%d%d" % (h, q) for q in range(nq)], [name], "b_sw")

    def look(t, h):
        a, b = slot(t + 1, h, r)
        return [lambda: ts(T.l0[:, cs(h)], T.psw[:, 64 * h:64 * h + 16], float(1021 * (t + 1)), A.add, ["lp%d" % h],
                           ["l0%d" % h], banks=["b_sw"]),
                lambda: ts(T.l1[:, cs(h)], T.l0[:, cs(h)], 4095, A.bitwise_and, ["l0%d" % h], ["l1%d" % h]),
                lambda: cp(T["lk%d" % (t + 1)][:, a:b], T.l1[:, cs(h)], ["l1%d" % h], ["lk%d%d_%d" % (t + 1, h, r)])]

    def keys(h):
        b = 64 * h + 16
        return [lambda: cp(T.kf[:, cs(h)], T.psw[:, b:b + 16], ["kp%d" % h], ["kf%d" % h], ["b_sw"]),
                lambda: ts(T.ki[:, cs(h)], T.psw[:, b + 16:b + 32], 256.0, A.mult, ["kp%d" % h], ["ki%d" % h], banks=["b_sw"]),
                lambda: ts(T.km[:, cs(h)], T.ki[:, cs(h)], 0xFFFF, A.bitwise_and, ["ki%d" % h], ["km%d" % h])]

    def colour_term(t, h):
        act(T.y1[:, hs(h)], T.kf[:, cs(h)].indirect(T.bo[:, 0:16]), ["kf%d" % h, "bo"], ["y1%d" % h], scale=101.0, bias=float(t))
        mm(ps("bb", h), ident, T.y1[:, hs(h)], False, True, ["y1%d" % h, "jf"], ["bb%d" % h], "b_bb%d" % h)

    def changes(h):
        return [lambda: tt(T.ui[:, hs(h)], T.km[:, cs(h)].indirect(T.bo[:, 0:16]), T.pw[:], A.mult,
                           ["km%d" % h, "bo"] + pw_all, ["ui%d" % h]),
                lambda: ts(T.ns[:, hs(h)], T.ui[:, hs(h)], 15, A.logical_shift_right, ["ui%d" % h], ["ns%d" % h], 1, A.bitwise_and)]

    def new_ends(h):
        pb = ps("bb", h)
        return [
            lambda: tt(pb, pb, T.ns[:, hs(h)], A.mult, ["bb%d" % h, "ns%d" % h], ["bb%d" % h], ["b_bb%d" % h]),
            lambda: tt(T.xi[:, hs(h)], pb, T.ef[:, hs(h)], A.add, ["bb%d" % h, "ef%d" % h], ["xi%d" % h], ["b_bb%d" % h]),
            lambda: ts(T.ei[:, hs(h)], T.xi[:, hs(h)], 4095, A.bitwise_and, ["xi%d" % h], ["ei%d" % h]),
            lambda: cp(T.nbu[:, hs(h)], T.ei[:, hs(h)], ["ei%d" % h], ["nbu%d" % h]),
            lambda: cp(T.ef[:, hs(h)], T.ei[:, hs(h)], ["ei%d" % h], ["ef%d" % h]),
            lambda: cp(T.yno[:, :, cs(h)], T.ei[:, hs(h)], ["ei%d" % h], ["yn%d" % h])]

    def results(h):
        return [lambda: cp(T.o1[:, cs(h)], T.kf[:, cs(h)], ["kf%d" % h], ["o1%d" % h]),
                lambda: ts(T.o2[:, cs(h)], T.o1[:, cs(h)], 4095, A.bitwise_and, ["o1%d" % h], ["o2%d" % h]),
                lambda: ts(T.o3[:, cs(h)], T.o1[:, cs(h)], 12, A.arith_shift_right, ["o1%d" % h], ["o3%d" % h]),
                lambda: cp(T.yco[:, cs(h)], T.o2[:, cs(h)], ["o2%d" % h], ["yc%d" % h]),
                lambda: ts(T.yxo[:, cs(h)], T.o3[:, cs(h)], 16.0, A.add, ["o3%d" % h], ["yx%d" % h])]

    d = [T.rank_of(c) for c in near]
    x = [T.rank_of(c) for c in far]
    table("S", 0, 0, r)
    own_columns(0)
    for h in range(2):
        open_sums(0, h)
        open_ends(h)
    for q, i in (("V", d[0]), ("S", d[1]), ("V", d[2]), ("S", x[0]), ("V", x[1]), ("S", x[2]), ("V", x[3])):
        table(q, 0, 0, i)
    for t in range(RO):
        sa, sb = NS_K[(t, 0)], NS_K[(t, 1)]
        gathers(t, 0, sa, 0, 8)
        ends(t, 0, sa, {}, 2)
        keep = []
        ka, kb, ca, cb, na, nb = keys(0), keys(1), changes(0), changes(1), new_ends(0), new_ends(1)
        gathers(t, 1, sb, 0, 2)
        if t < RO - 1:
            la, lb = look(t, 0), look(t, 1)
            cols = columns(t + 1, 0)
            first = [lambda: table("S", t + 1, 0, r), lambda: send(t + 1, 0)]
            ends(t, 1, sb, {1: [lambda: keep.append(least(0, 0)), lambda: keep.append(key2(0)), lambda: gathers(t, 1, sb, 2, 4),
                                lambda: keep[0](), lambda: back("lm", 0)],
                            3: [la[0]], 4: [la[1], la[2], lambda: keep[1]()] + (first if cols else first[1:])
                            + [lambda: gathers(t, 1, sb, 4, 8)]}, 1)
            s1b = least(1, 0)
            xb = key2(1)
            s1b()
            back("lm", 1)
            xb()
            least(0, 1)()
            lb[0]()
            back("sw", 0)
            steps(lb[1], lb[2])
            send(t + 1, 1)
            todo = [] if cols else [[0, 1], [2, 3], [4, 5], [6, 7]]
            for pair in todo[0:1]:
                table("S", t + 1, 0, pair[0], pair[1])
            s2b = least(1, 1)
            steps(ka[0], ka[1], s2b)
            back("sw", 1)
            colour_term(t, 0)
            for pair in todo[1:2]:
                table("S", t + 1, 0, pair[0], pair[1])
            steps(ka[2], ca[0], kb[0], kb[1], ca[1], kb[2])
            colour_term(t, 1)
            for pair in todo[2:]:
                table("S", t + 1, 0, pair[0], pair[1])
            table("S", t + 1, 1, r)
            own_columns(t + 1)
            for h in range(2):
                open_sums(t + 1, h)
            steps(na[0], cb[0], na[1], cb[1], na[2], nb[0], na[3], nb[1], na[4], nb[2], nb[3], nb[4])
            for i in d:
                table("S", t + 1, 1, i)
            for h in range(2):
                open_ends(h)
            for q, i in (("S", x[0]), ("V", x[1]), ("S", x[2]), ("V", x[3])):
                table(q, t + 1, 1, i)
        else:
            ra, rb = results(0), results(1)
            ends(t, 1, sb, {1: [lambda: keep.append(least(0, 0)), lambda: key2(0)(), lambda: gathers(t, 1, sb, 2, 4)],
                            2: [lambda: keep[0]()], 3: [lambda: keep.append(least(0, 1))],
                            4: [lambda: keep[1](), lambda: back("sw", 0)],
                            6: [ka[0], ka[1], lambda: colour_term(t, 0), lambda: gathers(t, 1, sb, 4, 8)],
                            7: [ka[2], ra[0]], 8: [ca[0], ra[1], ra[2]], 9: [ca[1], ra[3], ra[4]],
                            10: [na[0]], 11: [na[1]], 12: [na[2]]}, 1, True)
            na[5]()
            s1b = least(1, 0)
            s2b = least(1, 1)
            steps(s1b, s2b)
            back("sw", 1)
            steps(kb[0], kb[1])
            colour_term(t, 1)
            steps(rb[0], kb[2], rb[1], cb[0], rb[2], cb[1], rb[3], nb[0], rb[4], nb[1], nb[2], nb[5])
    op("SP", lambda: SP.dma_start(T.yn[:], T.yno[:]), ["yn0", "yn1"], ["on"], own=("dyn", 16))
    op("S", lambda: S.dma_start(T.yc[:], T.yco[:]), ["yc0", "yc1"], ["oc"], own=("dyc", 16))
    op("S", lambda: S.dma_start(T.yx[:], T.yxo[:]), ["yx0", "yx1"], ["ox"], own=("dyx", 16))
    op("SP", lambda: None, ["oc", "ox", "on"], [], own=("dyn", -1))
    run_ops(ops, outside, {"V": V, "S": S, "PE": PE, "G": g, "SP": SP}, T)
    g.wait_ge(T.sem.sent, sends[0])
